import numpy as np
import ml_dtypes


def mxq(x, axis, fmt="e4m3"):
    dtype, down = {"e4m3": (ml_dtypes.float8_e4m3fn, 7), "e5m2": (ml_dtypes.float8_e5m2, 14)}[fmt]
    v = np.moveaxis(np.asarray(x, np.float32).astype(ml_dtypes.bfloat16).astype(np.float64), axis, -1)
    blocks = v.reshape(v.shape[:-1] + (-1, 32))
    amax = np.abs(blocks).max(-1, keepdims=True)
    byte = np.maximum(np.where(amax > 0, np.frexp(amax)[1] - 1 + 127, 0) - down, 1)
    scale = np.exp2(byte - 127.0)
    codes = (blocks / scale).astype(np.float32).astype(dtype).astype(np.float64)
    return np.moveaxis((codes * scale).reshape(v.shape), -1, axis)


WIDE = False


def mx_kscale(k):
    if not WIDE:
        return np.ones(k)
    levels = np.array([10, -10, 5, -5, 0])
    if k % 512:
        return np.exp2(np.random.permutation(np.resize(levels, k // 32))).repeat(32)
    a = np.empty((k // 512, 16))
    for p in range(k // 512):
        a[p, :8] = np.random.permutation(np.resize(levels, 8))
        for g in range(8):
            far = levels[np.abs(levels - a[p, g]) >= 10]
            a[p, g + 8] = far[np.random.randint(len(far))]
    return np.exp2(a.ravel()).repeat(32)


def f64(x):
    return np.asarray(x).astype(np.float64)


def striped(idx):
    return np.tile(idx.reshape(-1, 16).T, (8, 1)).astype(np.uint16)


def unstriped(offs):
    return offs[:16].T.reshape(-1).astype(np.int64)


def striped8(idx):
    return np.concatenate([x.reshape(-1, 16).T for x in idx]).astype(np.uint16)


def runs(offs, k):
    lists = np.stack([offs[16 * r : 16 * r + 16].T.reshape(-1) for r in range(8)]).astype(np.int64)
    return lists[np.arange(k) % 512 // 64]


def pack_weight(w):
    k, n = w.shape
    w = f64(np.asarray(w, np.float32).astype(ml_dtypes.bfloat16)).reshape(k // 32, 32, n)
    amax = np.abs(w).max(1)
    byte = np.clip(np.where(amax > 0, np.frexp(amax)[1] - 1 + 127 - 7, 1), 1, 254)
    scaled = (w * np.exp2(127.0 - byte)[:, None, :]).reshape(k, n).astype(np.float32)
    words = np.ascontiguousarray(scaled.reshape(k // 512, 128, 4, n).transpose(0, 1, 3, 2)).astype(ml_dtypes.float8_e4m3fn).view(np.uint8)
    return words, np.ascontiguousarray(byte.astype(np.uint8).reshape(k // 512, 16, n))


def unpack_weight(words, scales):
    g, p, n, _ = words.shape
    vals = np.ascontiguousarray(words).view(ml_dtypes.float8_e4m3fn).astype(np.float64) * np.repeat(np.exp2(scales.astype(np.float64) - 127.0), 8, axis=1)[..., None]
    return vals.transpose(0, 1, 3, 2).reshape(g * 512, n)


E2M1 = np.array([0.0, 0.5, 1.0, 1.5, 2.0, 3.0, 4.0, 6.0, -0.0, -0.5, -1.0, -1.5, -2.0, -3.0, -4.0, -6.0])


def pack_fp4(w):
    k, n = w.shape
    w = f64(np.asarray(w, np.float32).astype(ml_dtypes.bfloat16)).reshape(k // 32, 32, n)
    amax = np.abs(w).max(1)
    mant, ex = np.frexp(amax / 6.0)
    byte = np.clip(np.where(amax > 0, np.where(mant > 0.5, ex, ex - 1) + 127, 1), 1, 254)
    scaled = (w * np.exp2(127.0 - byte)[:, None, :]).reshape(k, n).astype(np.float32)
    c = np.ascontiguousarray(scaled.reshape(k // 512, 128, 4, n).transpose(0, 1, 3, 2)).astype(ml_dtypes.float4_e2m1fn).view(np.uint8) & 0xF
    words = (c[..., 0::2] | (c[..., 1::2] << 4)).reshape(k // 512, 128, 2 * n)
    return np.ascontiguousarray(words), np.ascontiguousarray(byte.astype(np.uint8).reshape(k // 512, 16, n))


def unpack_fp4(words, scales):
    g, _, n = scales.shape
    words = np.ascontiguousarray(words).reshape(g, 128, n, 2)
    nib = np.empty((g, 128, n, 4), np.uint8)
    nib[..., 0::2] = words & 0xF
    nib[..., 1::2] = words >> 4
    vals = E2M1[nib] * np.repeat(np.exp2(scales.astype(np.float64) - 127.0), 8, axis=1)[..., None]
    return vals.transpose(0, 1, 3, 2).reshape(g * 512, n)


def planes(y):
    n, m = y.shape
    v = y.astype(np.float32).astype(ml_dtypes.bfloat16).astype(np.float64).reshape(n // 32, 32, m)
    top = np.abs(v).max(1)
    byte = np.clip(np.where(top > 0, np.frexp(top)[1] - 1 + 127 - 7, 1), 1, 254)
    codes = (v * np.exp2(127.0 - byte)[:, None, :]).reshape(n, m).astype(np.float32).astype(ml_dtypes.float8_e4m3fn).view(np.uint8)
    words = codes.reshape(n // 512, 128, 4, m).transpose(0, 1, 3, 2)
    return np.ascontiguousarray(words), np.ascontiguousarray(byte.astype(np.uint8).reshape(n // 512, 16, m))


K, T, S, N, H, U = 512, 2048, 512, 512, 512, 1024


def setup_inputs():
    n = np.random.standard_normal
    s = mx_kscale(K)[:, None]
    u = mx_kscale(H)
    packed_xT = pack_weight(n((K, T)) * s)
    packed_w1 = pack_fp4(n((K, H)) / np.sqrt(K) / s)
    packed_w2 = pack_fp4(n((H, N)) / np.sqrt(H) / u[:, None])
    return {
        "x_words": packed_xT[0],
        "x_scales": packed_xT[1],
        "w1_words": packed_w1[0],
        "w1_scales": packed_w1[1],
        "gn": (np.random.uniform(0.5, 1.5, (H, 1)) * u[:, None]).astype(np.float32),
        "w2_words": packed_w2[0],
        "w2_scales": packed_w2[1],
        "mem": n((N, U)).astype(np.float32),
        "offs": striped(np.random.permutation(T)[:S]),
        "n1": striped8(np.stack([np.random.permutation(S) for _ in range(8)])),
        "n2": striped8(np.stack([np.random.permutation(S) for _ in range(8)])),
        "n3": striped8(np.stack([np.random.permutation(U)[:S] for _ in range(8)])),
    }


def reference(x_words, x_scales, w1_words, w1_scales, gn, w2_words, w2_scales, mem, offs, n1, n2, n3):
    xq = unpack_weight(x_words, x_scales)[:, unstriped(offs)]
    y = unpack_fp4(w1_words, w1_scales).T @ xq
    st = y + 0.5 * (y[np.arange(H)[:, None], runs(n1, H)])
    z = f64(gn) * (st - (st[np.arange(H)[:, None], runs(n2, H)]))
    h = unpack_fp4(w2_words, w2_scales).T @ mxq(z, 0, "e4m3")
    nw = np.maximum(h, 0.5 * (f64(mem)[np.arange(N)[:, None], runs(n3, N)]))
    out = f64(mem).copy()
    out[np.arange(N)[:, None], runs(n3, N)] = nw
    return (out,) + planes(out)

@@ -1,0 +1,229 @@
+from contextlib import ExitStack
+
+import concourse.mybir as mybir
+
+K, T, S, H, N, U = 512, 2048, 512, 512, 512, 1024
+FLOPS = 2 * K * H * S + 2 * H * N * S
+
+F32 = mybir.dt.float32
+BF16 = mybir.dt.bfloat16
+I32 = mybir.dt.int32
+U32 = mybir.dt.uint32
+U16 = mybir.dt.uint16
+U8 = mybir.dt.uint8
+FP8X4 = mybir.dt.float8_e4m3fn_x4
+FP4X4 = mybir.dt.float4_e2m1fn_x4
+ALU = mybir.AluOpType
+COPY = mybir.ActivationFunctionType.Copy
+
+P = 128
+PACK = 4
+HALF = S // 2
+CHUNK = 256
+LANES = 16
+
+
+def tile_picked_layhoppagex_none_po_kernel(
+    tc, x_words, x_scales, w1_words, w1_scales, gn, w2_words, w2_scales, mem, offs, n1, n2, n3, out_0, out_1, out_2
+):
+    nc = tc.nc
+    with ExitStack() as ctx:
+        keep = ctx.enter_context(tc.tile_pool(name="keep", bufs=1))
+        psum = ctx.enter_context(tc.psum_pool(name="psum", bufs=1))
+
+        def sb(name, shape, dtype):
+            return keep.tile(shape, dtype, name=name, align_bytes=64)
+
+        def load_list(name, src):
+            lst = sb(name, [P, S // LANES], U16)
+            nc.sync.dma_start(lst[:], src)
+            return lst
+
+        def entries(lst, first, count):
+            return lst[:, first // LANES : (first + count) // LANES]
+
+        def load_scale_rows(name, src, width, queue):
+            plane = sb(name, [P, width], U8)
+            nc.vector.memset(plane[:].bitcast(I32), 0)
+            for q in range(4):
+                queue.dma_start(
+                    out=plane[32 * q : 32 * q + 4, :].bitcast(I32), in_=src[0, 4 * q : 4 * q + 4, :].bitcast(I32)
+                )
+            return plane
+
+        def load_fp4_words(name, src):
+            words = sb(name, [P, 2 * H], U8)
+            nc.sync.dma_start(out=words[:].bitcast(I32), in_=src[0].bitcast(I32))
+            return words
+
+        def deal_words(name, raw):
+            dealt = sb(name, [P, 2 * H], U8)
+            nc.vector.tensor_copy(
+                out=dealt[:].rearrange("p (t m b) -> p t m b", t=PACK, b=2),
+                in_=raw[:].rearrange("p (m t b) -> p t m b", t=PACK, b=2),
+            )
+            return dealt
+
+        def deal_scales(name, raw):
+            dealt = sb(name, [P, H], U8)
+            nc.vector.tensor_copy(
+                out=dealt[:].rearrange("p (t m) -> p t m", t=PACK),
+                in_=raw[:].rearrange("p (m t) -> p t m", t=PACK),
+            )
+            return dealt
+
+        def product(acc, words, scales, t, rhs_words, rhs_scales):
+            nc.tensor.matmul_mx(
+                out=acc,
+                lhsT=words[:, 2 * P * t : 2 * P * (t + 1)].bitcast(FP4X4),
+                lhsT_scale=scales[:, P * t : P * (t + 1)],
+                rhs=rhs_words.bitcast(FP8X4),
+                rhs_scale=rhs_scales,
+                start=True,
+                stop=True,
+            )
+
+        mem_rows = mem.rearrange("(p t) u -> p t u", t=PACK)
+        out_rows = out_0.rearrange("(p t) u -> p t u", t=PACK)
+
+        page = [sb("page%d" % t, [P, U], F32) for t in range(PACK)]
+        x_scale_rows = load_scale_rows("x_scale_rows", x_scales, T, nc.sync)
+        offs_sb = load_list("offs_sb", offs)
+        w1_raw = load_fp4_words("w1_raw", w1_words)
+        w2_raw = load_fp4_words("w2_raw", w2_words)
+        x_all = sb("x_all", [P, T], I32)
+        nc.sync.dma_start(out=x_all[:], in_=x_words[0].rearrange("p c r -> p (c r)").bitcast(I32))
+        w1_scale_rows = load_scale_rows("w1_scale_rows", w1_scales, H, nc.sync)
+        n3_sb = load_list("n3_sb", n3)
+        nc.sync.dma_start(out=page[0][:], in_=mem_rows[:, 0, :])
+        gain = sb("gain", [P, PACK], F32)
+        nc.sync.dma_start(out=gain[:], in_=gn.rearrange("(p t) o -> p (t o)", t=PACK))
+        n1_sb = load_list("n1_sb", n1)
+        nc.sync.dma_start(out=page[1][:], in_=mem_rows[:, 1, :])
+        n2_sb = load_list("n2_sb", n2)
+        w2_scale_rows = load_scale_rows("w2_scale_rows", w2_scales, N, nc.sync)
+        for t in (2, 3):
+            nc.sync.dma_start(out=page[t][:], in_=mem_rows[:, t, :])
+
+        half_gain = sb("half_gain", [P, PACK], F32)
+        nc.scalar.activation(out=half_gain[:], in_=gain[:], func=COPY, scale=0.5)
+
+        old = [sb("old%d" % t, [P, S], F32) for t in range(PACK)]
+
+        def fetch_old(t):
+            nc.vector.tensor_copy(old[t][:], page[t][:].indirect(n3_sb[:]))
+
+        w1_dealt = deal_words("w1_dealt", w1_raw)
+        picked_scales = sb("picked_scales", [P, S], U8)
+        nc.vector.tensor_copy(picked_scales[:], x_scale_rows[:].indirect(offs_sb[:]))
+        w2_dealt = deal_words("w2_dealt", w2_raw)
+        picked_words = sb("picked_words", [P, S], U32)
+        nc.vector.tensor_copy(picked_words[:], x_all[:].bitcast(U32).indirect(offs_sb[:]))
+        w1_scale_dealt = deal_scales("w1_scale_dealt", w1_scale_rows)
+
+        y_full, y_half = [], []
+        for t in range(PACK):
+            y = psum.tile([P, S], F32, name="y%d" % t, tag="bank%d" % t)
+            product(y[:], w1_dealt, w1_scale_dealt, t, picked_words[:], picked_scales[:])
+            y_half.append(sb("y_half%d" % t, [P, S], F32))
+            y_full.append(sb("y_full%d" % t, [P, S], F32))
+            nc.scalar.activation(out=y_half[t][:], in_=y[:], func=COPY, scale=half_gain[:, t : t + 1])
+            nc.scalar.activation(out=y_full[t][:], in_=y[:], func=COPY, scale=gain[:, t : t + 1])
+
+        fetch_old(0)
+        fetch_old(1)
+        w2_scale_dealt = deal_scales("w2_scale_dealt", w2_scale_rows)
+
+        st, st_copy = [], []
+        for t in range(PACK):
+            st.append(sb("st%d" % t, [P, S], F32))
+            for h in range(2):
+                cols = slice(HALF * h, HALF * (h + 1))
+                nc.vector.tensor_tensor(
+                    st[t][:, cols], y_half[t][:].indirect(entries(n1_sb, HALF * h, HALF)), y_full[t][:, cols], ALU.add
+                )
+        for t in range(PACK):
+            st_copy.append(sb("st_copy%d" % t, [P, S], F32))
+            nc.scalar.copy(out=st_copy[t][:], in_=st[t][:])
+
+        z_bf16 = []
+        for h in range(2):
+            cols = slice(HALF * h, HALF * (h + 1))
+            minus_z = sb("minus_z%d" % h, [P, PACK, HALF], F32)
+            for t in range(PACK):
+                nc.vector.tensor_tensor(
+                    minus_z[:, t, :], st[t][:].indirect(entries(n2_sb, HALF * h, HALF)), st_copy[t][:, cols], ALU.subtract
+                )
+            z_bf16.append(sb("z_bf16_%d" % h, [P, HALF * PACK], BF16))
+            nc.scalar.activation(
+                out=z_bf16[h][:].rearrange("p (c i t) -> p c t i", i=4, t=PACK),
+                in_=minus_z[:].rearrange("p t (c i) -> p c t i", i=4),
+                func=COPY,
+                scale=-1.0,
+            )
+
+        hid = {}
+
+        def second_product(h):
+            z_words = sb("z_words%d" % h, [P, HALF], U32)
+            z_scales = sb("z_scales%d" % h, [P, HALF], U8)
+            nc.vector.quantize_mx(out=z_words[:].bitcast(FP8X4), scales=z_scales[:], in_=z_bf16[h][:])
+            for t in range(PACK):
+                hid[t, h] = psum.tile([P, HALF], F32, name="hid%d_%d" % (t, h), tag="bank%d" % (PACK * (1 - h) + t))
+                product(hid[t, h][:], w2_dealt, w2_scale_dealt, t, z_words[:], z_scales[:])
+
+        new = [sb("new%d" % t, [P, S], F32) for t in range(PACK)]
+
+        def larger(t, h):
+            cols = slice(HALF * h, HALF * (h + 1))
+            nc.vector.scalar_tensor_tensor(
+                out=new[t][:, cols], in0=old[t][:, cols], scalar=0.5, in1=hid[t, h][:], op0=ALU.mult, op1=ALU.max
+            )
+
+        chunks = U // CHUNK
+        pairs = [sb("pairs%d" % k, [P, 2, CHUNK, 2], BF16) for k in range(chunks)]
+
+        def finish(t):
+            nc.vector.tensor_copy(page[t][:].indirect(n3_sb[:]), new[t][:])
+            nc.sync.dma_start(out=out_rows[:, t, :], in_=page[t][:])
+            for k in range(chunks):
+                nc.scalar.copy(out=pairs[k][:, t // 2, :, t % 2], in_=page[t][:, CHUNK * k : CHUNK * (k + 1)])
+
+        second_product(0)
+        fetch_old(2)
+        for t in range(3):
+            larger(t, 0)
+        second_product(1)
+        fetch_old(3)
+        larger(3, 0)
+        for t in range(PACK):
+            larger(t, 1)
+            finish(t)
+
+        out_words = out_1[0].rearrange("p c r -> p (c r)").bitcast(I32)
+        scale_plane = sb("scale_plane", [P, U], U8)
+        woven = []
+        for k in range(chunks):
+            woven.append(sb("woven%d" % k, [P, CHUNK * PACK], BF16))
+
+        def weave(k):
+            nc.vector.tensor_copy(
+                out=woven[k][:].bitcast(I32).rearrange("p (c u) -> p c u", u=2),
+                in_=pairs[k][:].rearrange("p u c e -> p u (c e)").bitcast(I32).rearrange("p u c -> p c u"),
+            )
+
+        def emit(k):
+            cols = slice(CHUNK * k, CHUNK * (k + 1))
+            codes = sb("codes%d" % k, [P, CHUNK], I32)
+            nc.vector.quantize_mx(out=codes[:].bitcast(FP8X4), scales=scale_plane[:, cols], in_=woven[k][:])
+            nc.sync.dma_start(out=out_words[:, cols], in_=codes[:])
+
+        weave(0)
+        for k in range(chunks):
+            if k + 1 < chunks:
+                weave(k + 1)
+            emit(k)
+        for q in range(4):
+            nc.scalar.dma_start(
+                out=out_2[0, 4 * q : 4 * q + 4, :].bitcast(I32), in_=scale_plane[32 * q : 32 * q + 4, :].bitcast(I32)
+            )

@@ -31,16 +31,13 @@ def tile_picked_layhoppagex_none_po_kernel(
         keep = ctx.enter_context(tc.tile_pool(name="keep", bufs=1))
         psum = ctx.enter_context(tc.psum_pool(name="psum", bufs=1))
 
-        def sb(name, shape, dtype):
-            return keep.tile(shape, dtype, name=name, align_bytes=64)
+        def sb(name, shape, dtype, tag=None):
+            return keep.tile(shape, dtype, name=name, tag=tag or name, align_bytes=64)
 
         def load_list(name, src):
             lst = sb(name, [P, S // LANES], U16)
             nc.sync.dma_start(lst[:], src)
             return lst
-
-        def entries(lst, first, count):
-            return lst[:, first // LANES : (first + count) // LANES]
 
         def load_scale_rows(name, src, width, queue):
             plane = sb(name, [P, width], U8)
@@ -99,18 +96,19 @@ def tile_picked_layhoppagex_none_po_kernel(
         gain = sb("gain", [P, PACK], F32)
         nc.sync.dma_start(out=gain[:], in_=gn.rearrange("(p t) o -> p (t o)", t=PACK))
         n1_sb = load_list("n1_sb", n1)
-        nc.sync.dma_start(out=page[1][:], in_=mem_rows[:, 1, :])
+        nc.sync.dma_start(out=page[2][:], in_=mem_rows[:, 2, :])
         n2_sb = load_list("n2_sb", n2)
         w2_scale_rows = load_scale_rows("w2_scale_rows", w2_scales, N, nc.sync)
-        for t in (2, 3):
+        for t in (1, 3):
             nc.sync.dma_start(out=page[t][:], in_=mem_rows[:, t, :])
 
         half_gain = sb("half_gain", [P, PACK], F32)
         nc.scalar.activation(out=half_gain[:], in_=gain[:], func=COPY, scale=0.5)
 
-        old = [sb("old%d" % t, [P, S], F32) for t in range(PACK)]
+        old = {}
 
-        def fetch_old(t):
+        def fetch_old(t, tag=None):
+            old[t] = sb("old%d" % t, [P, S], F32, tag)
             nc.vector.tensor_copy(old[t][:], page[t][:].indirect(n3_sb[:]))
 
         w1_dealt = deal_words("w1_dealt", w1_raw)
@@ -121,108 +119,111 @@ def tile_picked_layhoppagex_none_po_kernel(
         nc.vector.tensor_copy(picked_words[:], x_all[:].bitcast(U32).indirect(offs_sb[:]))
         w1_scale_dealt = deal_scales("w1_scale_dealt", w1_scale_rows)
 
-        y_full, y_half = [], []
+        hop_window = [sb("hop_window%d" % t, [P, 2 * S], F32) for t in range(PACK)]
+        st_window = [sb("st_window%d" % t, [P, 2 * S], F32) for t in range(PACK)]
+        last_copy = sb("last_copy", [P, S], F32)
+        nc.vector.memset(hop_window[0][:, S:], 0.0)
+        y_full = [hop_window[t + 1][:, S:] for t in range(PACK - 1)] + [st_window[0][:, S:]]
+        st_copy = [st_window[t + 1][:, S:] for t in range(PACK - 1)] + [last_copy[:]]
         for t in range(PACK):
             y = psum.tile([P, S], F32, name="y%d" % t, tag="bank%d" % t)
             product(y[:], w1_dealt, w1_scale_dealt, t, picked_words[:], picked_scales[:])
-            y_half.append(sb("y_half%d" % t, [P, S], F32))
-            y_full.append(sb("y_full%d" % t, [P, S], F32))
-            nc.scalar.activation(out=y_half[t][:], in_=y[:], func=COPY, scale=half_gain[:, t : t + 1])
-            nc.scalar.activation(out=y_full[t][:], in_=y[:], func=COPY, scale=gain[:, t : t + 1])
+            nc.scalar.activation(out=hop_window[t][:, :S], in_=y[:], func=COPY, scale=half_gain[:, t : t + 1])
+            nc.scalar.activation(out=y_full[t], in_=y[:], func=COPY, scale=gain[:, t : t + 1])
 
         fetch_old(0)
-        fetch_old(1)
         w2_scale_dealt = deal_scales("w2_scale_dealt", w2_scale_rows)
+        fetch_old(2)
 
-        st, st_copy = [], []
         for t in range(PACK):
-            st.append(sb("st%d" % t, [P, S], F32))
-            for h in range(2):
-                cols = slice(HALF * h, HALF * (h + 1))
-                nc.vector.tensor_tensor(
-                    st[t][:, cols], y_half[t][:].indirect(entries(n1_sb, HALF * h, HALF)), y_full[t][:, cols], ALU.add
-                )
+            nc.vector.tensor_tensor(st_window[t][:, :S], hop_window[t][:].indirect(n1_sb[:]), y_full[t], ALU.add)
         for t in range(PACK):
-            st_copy.append(sb("st_copy%d" % t, [P, S], F32))
-            nc.scalar.copy(out=st_copy[t][:], in_=st[t][:])
+            nc.scalar.copy(out=st_copy[t], in_=st_window[t][:, :S])
 
+        minus_z = sb("minus_z", [P, PACK, S], F32)
+        for t in range(PACK):
+            nc.vector.tensor_tensor(minus_z[:, t, :], st_window[t][:].indirect(n2_sb[:]), st_copy[t], ALU.subtract)
         z_bf16 = []
         for h in range(2):
-            cols = slice(HALF * h, HALF * (h + 1))
-            minus_z = sb("minus_z%d" % h, [P, PACK, HALF], F32)
-            for t in range(PACK):
-                nc.vector.tensor_tensor(
-                    minus_z[:, t, :], st[t][:].indirect(entries(n2_sb, HALF * h, HALF)), st_copy[t][:, cols], ALU.subtract
-                )
             z_bf16.append(sb("z_bf16_%d" % h, [P, HALF * PACK], BF16))
             nc.scalar.activation(
                 out=z_bf16[h][:].rearrange("p (c i t) -> p c t i", i=4, t=PACK),
-                in_=minus_z[:].rearrange("p t (c i) -> p c t i", i=4),
+                in_=minus_z[:, :, HALF * h : HALF * (h + 1)].rearrange("p t (c i) -> p c t i", i=4),
                 func=COPY,
                 scale=-1.0,
             )
 
+        order = (2, 0, 1, 3)
+        last = order[-1]
         hid = {}
+        hid_last = psum.tile([P, S], F32, name="hid_last", tag="bank7")
 
         def second_product(h):
             z_words = sb("z_words%d" % h, [P, HALF], U32)
             z_scales = sb("z_scales%d" % h, [P, HALF], U8)
             nc.vector.quantize_mx(out=z_words[:].bitcast(FP8X4), scales=z_scales[:], in_=z_bf16[h][:])
-            for t in range(PACK):
-                hid[t, h] = psum.tile([P, HALF], F32, name="hid%d_%d" % (t, h), tag="bank%d" % (PACK * (1 - h) + t))
-                product(hid[t, h][:], w2_dealt, w2_scale_dealt, t, z_words[:], z_scales[:])
+            for t in order:
+                if t == last:
+                    acc = hid_last[:, HALF * h : HALF * (h + 1)]
+                else:
+                    hid[t, h] = psum.tile([P, HALF], F32, name="hid%d_%d" % (t, h), tag="bank%d" % (PACK * (1 - h) + t))
+                    acc = hid[t, h][:]
+                product(acc, w2_dealt, w2_scale_dealt, t, z_words[:], z_scales[:])
 
-        new = [sb("new%d" % t, [P, S], F32) for t in range(PACK)]
+        def larger(dst, held, acc):
+            nc.vector.scalar_tensor_tensor(out=dst, in0=held, scalar=0.5, in1=acc, op0=ALU.mult, op1=ALU.max)
 
-        def larger(t, h):
+        def larger_half(t, h):
             cols = slice(HALF * h, HALF * (h + 1))
-            nc.vector.scalar_tensor_tensor(
-                out=new[t][:, cols], in0=old[t][:, cols], scalar=0.5, in1=hid[t, h][:], op0=ALU.mult, op1=ALU.max
-            )
+            larger(new[t][:, cols], old[t][:, cols], hid[t, h][:])
 
         chunks = U // CHUNK
-        pairs = [sb("pairs%d" % k, [P, 2, CHUNK, 2], BF16) for k in range(chunks)]
+        woven = [sb("woven%d" % k, [P, CHUNK, PACK], BF16) for k in range(chunks)]
 
-        def finish(t):
-            nc.vector.tensor_copy(page[t][:].indirect(n3_sb[:]), new[t][:])
+        def put(t):
+            nc.vector.tensor_copy(page[t][:].indirect(n3_sb[:]), new[t])
+
+        def hand_out(t):
             nc.sync.dma_start(out=out_rows[:, t, :], in_=page[t][:])
             for k in range(chunks):
-                nc.scalar.copy(out=pairs[k][:, t // 2, :, t % 2], in_=page[t][:, CHUNK * k : CHUNK * (k + 1)])
+                cols = slice(CHUNK * k, CHUNK * (k + 1))
+                if t == PACK - 1 and k < chunks // 2:
+                    nc.vector.tensor_copy(out=woven[k][:, :, t], in_=page[t][:, cols])
+                else:
+                    nc.scalar.copy(out=woven[k][:, :, t], in_=page[t][:, cols])
 
+        fetch_old(1, "last_copy")
         second_product(0)
-        fetch_old(2)
-        for t in range(3):
-            larger(t, 0)
+        fetch_old(3, "z_bf16_0")
         second_product(1)
-        fetch_old(3)
-        larger(3, 0)
-        for t in range(PACK):
-            larger(t, 1)
-            finish(t)
+        new_first = sb("new_first", [P, PACK - 1, S], F32, "z_bf16_1")
+        new = {t: new_first[:, t, :] for t in order[:-1]}
+        for t in order[:-1]:
+            larger_half(t, 0)
+        larger_half(2, 1)
+        larger_half(0, 1)
+        put(2)
+        hand_out(2)
+        larger_half(1, 1)
+        put(0)
+        hand_out(0)
+        put(1)
+        hand_out(1)
+        new_last = sb("new_last", [P, S], F32, "page2")
+        new[last] = new_last[:]
+        larger(new[last], old[last][:], hid_last[:])
+        put(last)
+        hand_out(last)
 
         out_words = out_1[0].rearrange("p c r -> p (c r)").bitcast(I32)
         scale_plane = sb("scale_plane", [P, U], U8)
-        woven = []
         for k in range(chunks):
-            woven.append(sb("woven%d" % k, [P, CHUNK * PACK], BF16))
-
-        def weave(k):
-            nc.vector.tensor_copy(
-                out=woven[k][:].bitcast(I32).rearrange("p (c u) -> p c u", u=2),
-                in_=pairs[k][:].rearrange("p u c e -> p u (c e)").bitcast(I32).rearrange("p u c -> p c u"),
-            )
-
-        def emit(k):
             cols = slice(CHUNK * k, CHUNK * (k + 1))
             codes = sb("codes%d" % k, [P, CHUNK], I32)
-            nc.vector.quantize_mx(out=codes[:].bitcast(FP8X4), scales=scale_plane[:, cols], in_=woven[k][:])
+            nc.vector.quantize_mx(
+                out=codes[:].bitcast(FP8X4), scales=scale_plane[:, cols], in_=woven[k][:].rearrange("p c t -> p (c t)")
+            )
             nc.sync.dma_start(out=out_words[:, cols], in_=codes[:])
-
-        weave(0)
-        for k in range(chunks):
-            if k + 1 < chunks:
-                weave(k + 1)
-            emit(k)
         for q in range(4):
             nc.scalar.dma_start(
                 out=out_2[0, 4 * q : 4 * q + 4, :].bitcast(I32), in_=scale_plane[32 * q : 32 * q + 4, :].bitcast(I32)

@@ -120,11 +120,9 @@ def tile_picked_layhoppagex_none_po_kernel(
         w1_scale_dealt = deal_scales("w1_scale_dealt", w1_scale_rows)
 
         hop_window = [sb("hop_window%d" % t, [P, 2 * S], F32) for t in range(PACK)]
-        st_window = [sb("st_window%d" % t, [P, 2 * S], F32) for t in range(PACK)]
-        last_copy = sb("last_copy", [P, S], F32)
+        last_full = sb("last_full", [P, S], F32)
         nc.vector.memset(hop_window[0][:, S:], 0.0)
-        y_full = [hop_window[t + 1][:, S:] for t in range(PACK - 1)] + [st_window[0][:, S:]]
-        st_copy = [st_window[t + 1][:, S:] for t in range(PACK - 1)] + [last_copy[:]]
+        y_full = [hop_window[t + 1][:, S:] for t in range(PACK - 1)] + [last_full[:]]
         for t in range(PACK):
             y = psum.tile([P, S], F32, name="y%d" % t, tag="bank%d" % t)
             product(y[:], w1_dealt, w1_scale_dealt, t, picked_words[:], picked_scales[:])
@@ -134,21 +132,28 @@ def tile_picked_layhoppagex_none_po_kernel(
         fetch_old(0)
         w2_scale_dealt = deal_scales("w2_scale_dealt", w2_scale_rows)
         fetch_old(2)
+        fetch_old(1)
 
+        st = [sb("st%d" % t, [P, S], F32) for t in range(PACK)]
+        st_copy = [sb("st_copy%d" % t, [P, S], F32) for t in range(PACK)]
         for t in range(PACK):
-            nc.vector.tensor_tensor(st_window[t][:, :S], hop_window[t][:].indirect(n1_sb[:]), y_full[t], ALU.add)
-        for t in range(PACK):
-            nc.scalar.copy(out=st_copy[t], in_=st_window[t][:, :S])
+            nc.vector.tensor_tensor(st[t][:], hop_window[t][:].indirect(n1_sb[:]), y_full[t], ALU.add)
+        for h in range(2):
+            for t in range(PACK):
+                cols = slice(HALF * h, HALF * (h + 1))
+                nc.scalar.copy(out=st_copy[t][:, cols], in_=st[t][:, cols])
 
-        minus_z = sb("minus_z", [P, PACK, S], F32)
-        for t in range(PACK):
-            nc.vector.tensor_tensor(minus_z[:, t, :], st_window[t][:].indirect(n2_sb[:]), st_copy[t], ALU.subtract)
         z_bf16 = []
         for h in range(2):
+            cols = slice(HALF * h, HALF * (h + 1))
+            half_list = n2_sb[:, HALF * h // LANES : HALF * (h + 1) // LANES]
+            minus_z = sb("minus_z%d" % h, [P, PACK, HALF], F32)
+            for t in range(PACK):
+                nc.vector.tensor_tensor(minus_z[:, t, :], st[t][:].indirect(half_list), st_copy[t][:, cols], ALU.subtract)
             z_bf16.append(sb("z_bf16_%d" % h, [P, HALF * PACK], BF16))
             nc.scalar.activation(
                 out=z_bf16[h][:].rearrange("p (c i t) -> p c t i", i=4, t=PACK),
-                in_=minus_z[:, :, HALF * h : HALF * (h + 1)].rearrange("p t (c i) -> p c t i", i=4),
+                in_=minus_z[:].rearrange("p t (c i) -> p c t i", i=4),
                 func=COPY,
                 scale=-1.0,
             )
@@ -192,11 +197,10 @@ def tile_picked_layhoppagex_none_po_kernel(
                 else:
                     nc.scalar.copy(out=woven[k][:, :, t], in_=page[t][:, cols])
 
-        fetch_old(1, "last_copy")
         second_product(0)
-        fetch_old(3, "z_bf16_0")
+        fetch_old(3, "minus_z0")
         second_product(1)
-        new_first = sb("new_first", [P, PACK - 1, S], F32, "z_bf16_1")
+        new_first = sb("new_first", [P, PACK - 1, S], F32, "minus_z1")
         new = {t: new_first[:, t, :] for t in order[:-1]}
         for t in order[:-1]:
             larger_half(t, 0)

from contextlib import ExitStack

import concourse.mybir as mybir

K, T, S, H, N, U = 512, 2048, 512, 512, 512, 1024
FLOPS = 2 * K * H * S + 2 * H * N * S

F32 = mybir.dt.float32
BF16 = mybir.dt.bfloat16
I32 = mybir.dt.int32
U32 = mybir.dt.uint32
U16 = mybir.dt.uint16
U8 = mybir.dt.uint8
FP8X4 = mybir.dt.float8_e4m3fn_x4
FP4X4 = mybir.dt.float4_e2m1fn_x4
ALU = mybir.AluOpType
COPY = mybir.ActivationFunctionType.Copy

P = 128
PACK = 4
HALF = S // 2
CHUNK = 256
LANES = 16


def tile_picked_layhoppagex_none_po_kernel(
    tc, x_words, x_scales, w1_words, w1_scales, gn, w2_words, w2_scales, mem, offs, n1, n2, n3, out_0, out_1, out_2
):
    nc = tc.nc
    with ExitStack() as ctx:
        keep = ctx.enter_context(tc.tile_pool(name="keep", bufs=1))
        psum = ctx.enter_context(tc.psum_pool(name="psum", bufs=1))

        def sb(name, shape, dtype, tag=None):
            return keep.tile(shape, dtype, name=name, tag=tag or name, align_bytes=64)

        def load_list(name, src):
            lst = sb(name, [P, S // LANES], U16)
            nc.sync.dma_start(lst[:], src)
            return lst

        def load_scale_rows(name, src, width, queue):
            plane = sb(name, [P, width], U8)
            nc.vector.memset(plane[:].bitcast(I32), 0)
            for q in range(4):
                queue.dma_start(
                    out=plane[32 * q : 32 * q + 4, :].bitcast(I32), in_=src[0, 4 * q : 4 * q + 4, :].bitcast(I32)
                )
            return plane

        def load_fp4_words(name, src):
            words = sb(name, [P, 2 * H], U8)
            nc.sync.dma_start(out=words[:].bitcast(I32), in_=src[0].bitcast(I32))
            return words

        def deal_words(name, raw):
            dealt = sb(name, [P, 2 * H], U8)
            nc.vector.tensor_copy(
                out=dealt[:].rearrange("p (t m b) -> p t m b", t=PACK, b=2),
                in_=raw[:].rearrange("p (m t b) -> p t m b", t=PACK, b=2),
            )
            return dealt

        def deal_scales(name, raw):
            dealt = sb(name, [P, H], U8)
            nc.vector.tensor_copy(
                out=dealt[:].rearrange("p (t m) -> p t m", t=PACK),
                in_=raw[:].rearrange("p (m t) -> p t m", t=PACK),
            )
            return dealt

        def product(acc, words, scales, t, rhs_words, rhs_scales):
            nc.tensor.matmul_mx(
                out=acc,
                lhsT=words[:, 2 * P * t : 2 * P * (t + 1)].bitcast(FP4X4),
                lhsT_scale=scales[:, P * t : P * (t + 1)],
                rhs=rhs_words.bitcast(FP8X4),
                rhs_scale=rhs_scales,
                start=True,
                stop=True,
            )

        mem_rows = mem.rearrange("(p t) u -> p t u", t=PACK)
        out_rows = out_0.rearrange("(p t) u -> p t u", t=PACK)

        page = [sb("page%d" % t, [P, U], F32) for t in range(PACK)]
        x_scale_rows = load_scale_rows("x_scale_rows", x_scales, T, nc.sync)
        offs_sb = load_list("offs_sb", offs)
        w1_raw = load_fp4_words("w1_raw", w1_words)
        w2_raw = load_fp4_words("w2_raw", w2_words)
        x_all = sb("x_all", [P, T], I32)
        nc.sync.dma_start(out=x_all[:], in_=x_words[0].rearrange("p c r -> p (c r)").bitcast(I32))
        w1_scale_rows = load_scale_rows("w1_scale_rows", w1_scales, H, nc.sync)
        n3_sb = load_list("n3_sb", n3)
        nc.sync.dma_start(out=page[0][:], in_=mem_rows[:, 0, :])
        gain = sb("gain", [P, PACK], F32)
        nc.sync.dma_start(out=gain[:], in_=gn.rearrange("(p t) o -> p (t o)", t=PACK))
        n1_sb = load_list("n1_sb", n1)
        nc.sync.dma_start(out=page[2][:], in_=mem_rows[:, 2, :])
        n2_sb = load_list("n2_sb", n2)
        w2_scale_rows = load_scale_rows("w2_scale_rows", w2_scales, N, nc.sync)
        for t in (1, 3):
            nc.sync.dma_start(out=page[t][:], in_=mem_rows[:, t, :])

        half_gain = sb("half_gain", [P, PACK], F32)
        nc.scalar.activation(out=half_gain[:], in_=gain[:], func=COPY, scale=0.5)

        old = {}

        def fetch_old(t, tag=None):
            old[t] = sb("old%d" % t, [P, S], F32, tag)
            nc.vector.tensor_copy(old[t][:], page[t][:].indirect(n3_sb[:]))

        w1_dealt = deal_words("w1_dealt", w1_raw)
        picked_scales = sb("picked_scales", [P, S], U8)
        nc.vector.tensor_copy(picked_scales[:], x_scale_rows[:].indirect(offs_sb[:]))
        w2_dealt = deal_words("w2_dealt", w2_raw)
        picked_words = sb("picked_words", [P, S], U32)
        nc.vector.tensor_copy(picked_words[:], x_all[:].bitcast(U32).indirect(offs_sb[:]))
        w1_scale_dealt = deal_scales("w1_scale_dealt", w1_scale_rows)

        hop_window = [sb("hop_window%d" % t, [P, 2 * S], F32) for t in range(PACK)]
        last_full = sb("last_full", [P, S], F32)
        nc.vector.memset(hop_window[0][:, S:], 0.0)
        y_full = [hop_window[t + 1][:, S:] for t in range(PACK - 1)] + [last_full[:]]
        for t in range(PACK):
            y = psum.tile([P, S], F32, name="y%d" % t, tag="bank%d" % t)
            product(y[:], w1_dealt, w1_scale_dealt, t, picked_words[:], picked_scales[:])
            nc.scalar.activation(out=hop_window[t][:, :S], in_=y[:], func=COPY, scale=half_gain[:, t : t + 1])
            nc.scalar.activation(out=y_full[t], in_=y[:], func=COPY, scale=gain[:, t : t + 1])

        fetch_old(0)
        w2_scale_dealt = deal_scales("w2_scale_dealt", w2_scale_rows)
        fetch_old(2)
        fetch_old(1)

        st = [sb("st%d" % t, [P, S], F32) for t in range(PACK)]
        st_copy = [sb("st_copy%d" % t, [P, S], F32) for t in range(PACK)]
        for t in range(PACK):
            nc.vector.tensor_tensor(st[t][:], hop_window[t][:].indirect(n1_sb[:]), y_full[t], ALU.add)
        for h in range(2):
            for t in range(PACK):
                cols = slice(HALF * h, HALF * (h + 1))
                nc.scalar.copy(out=st_copy[t][:, cols], in_=st[t][:, cols])

        z_bf16 = []
        for h in range(2):
            cols = slice(HALF * h, HALF * (h + 1))
            half_list = n2_sb[:, HALF * h // LANES : HALF * (h + 1) // LANES]
            minus_z = sb("minus_z%d" % h, [P, PACK, HALF], F32)
            for t in range(PACK):
                nc.vector.tensor_tensor(minus_z[:, t, :], st[t][:].indirect(half_list), st_copy[t][:, cols], ALU.subtract)
            z_bf16.append(sb("z_bf16_%d" % h, [P, HALF * PACK], BF16))
            nc.scalar.activation(
                out=z_bf16[h][:].rearrange("p (c i t) -> p c t i", i=4, t=PACK),
                in_=minus_z[:].rearrange("p t (c i) -> p c t i", i=4),
                func=COPY,
                scale=-1.0,
            )

        order = (2, 0, 1, 3)
        last = order[-1]
        hid = {}
        hid_last = psum.tile([P, S], F32, name="hid_last", tag="bank7")

        def second_product(h):
            z_words = sb("z_words%d" % h, [P, HALF], U32)
            z_scales = sb("z_scales%d" % h, [P, HALF], U8)
            nc.vector.quantize_mx(out=z_words[:].bitcast(FP8X4), scales=z_scales[:], in_=z_bf16[h][:])
            for t in order:
                if t == last:
                    acc = hid_last[:, HALF * h : HALF * (h + 1)]
                else:
                    hid[t, h] = psum.tile([P, HALF], F32, name="hid%d_%d" % (t, h), tag="bank%d" % (PACK * (1 - h) + t))
                    acc = hid[t, h][:]
                product(acc, w2_dealt, w2_scale_dealt, t, z_words[:], z_scales[:])

        def larger(dst, held, acc):
            nc.vector.scalar_tensor_tensor(out=dst, in0=held, scalar=0.5, in1=acc, op0=ALU.mult, op1=ALU.max)

        def larger_half(t, h):
            cols = slice(HALF * h, HALF * (h + 1))
            larger(new[t][:, cols], old[t][:, cols], hid[t, h][:])

        chunks = U // CHUNK
        woven = [sb("woven%d" % k, [P, CHUNK, PACK], BF16) for k in range(chunks)]

        def put(t):
            nc.vector.tensor_copy(page[t][:].indirect(n3_sb[:]), new[t])

        def hand_out(t):
            nc.sync.dma_start(out=out_rows[:, t, :], in_=page[t][:])
            for k in range(chunks):
                cols = slice(CHUNK * k, CHUNK * (k + 1))
                if t == PACK - 1 and k < chunks // 2:
                    nc.vector.tensor_copy(out=woven[k][:, :, t], in_=page[t][:, cols])
                else:
                    nc.scalar.copy(out=woven[k][:, :, t], in_=page[t][:, cols])

        second_product(0)
        fetch_old(3, "minus_z0")
        second_product(1)
        new_first = sb("new_first", [P, PACK - 1, S], F32, "minus_z1")
        new = {t: new_first[:, t, :] for t in order[:-1]}
        for t in order[:-1]:
            larger_half(t, 0)
        larger_half(2, 1)
        larger_half(0, 1)
        put(2)
        hand_out(2)
        larger_half(1, 1)
        put(0)
        hand_out(0)
        put(1)
        hand_out(1)
        new_last = sb("new_last", [P, S], F32, "page2")
        new[last] = new_last[:]
        larger(new[last], old[last][:], hid_last[:])
        put(last)
        hand_out(last)

        out_words = out_1[0].rearrange("p c r -> p (c r)").bitcast(I32)
        scale_plane = sb("scale_plane", [P, U], U8)
        for k in range(chunks):
            cols = slice(CHUNK * k, CHUNK * (k + 1))
            codes = sb("codes%d" % k, [P, CHUNK], I32)
            nc.vector.quantize_mx(
                out=codes[:].bitcast(FP8X4), scales=scale_plane[:, cols], in_=woven[k][:].rearrange("p c t -> p (c t)")
            )
            nc.sync.dma_start(out=out_words[:, cols], in_=codes[:])
        for q in range(4):
            nc.scalar.dma_start(
                out=out_2[0, 4 * q : 4 * q + 4, :].bitcast(I32), in_=scale_plane[32 * q : 32 * q + 4, :].bitcast(I32)
            )
